import numpy as np
import ml_dtypes


def mxq(x, axis, fmt="e4m3"):
    dtype, down = {"e4m3": (ml_dtypes.float8_e4m3fn, 7), "e5m2": (ml_dtypes.float8_e5m2, 14)}[fmt]
    v = np.moveaxis(np.asarray(x, np.float32).astype(ml_dtypes.bfloat16).astype(np.float64), axis, -1)
    blocks = v.reshape(v.shape[:-1] + (-1, 32))
    amax = np.abs(blocks).max(-1, keepdims=True)
    byte = np.maximum(np.where(amax > 0, np.frexp(amax)[1] - 1 + 127, 0) - down, 1)
    scale = np.exp2(byte - 127.0)
    codes = (blocks / scale).astype(np.float32).astype(dtype).astype(np.float64)
    return np.moveaxis((codes * scale).reshape(v.shape), -1, axis)


WIDE = False


def mx_kscale(k):
    if not WIDE:
        return np.ones(k)
    levels = np.array([10, -10, 5, -5, 0])
    if k % 512:
        return np.exp2(np.random.permutation(np.resize(levels, k // 32))).repeat(32)
    a = np.empty((k // 512, 16))
    for p in range(k // 512):
        a[p, :8] = np.random.permutation(np.resize(levels, 8))
        for g in range(8):
            far = levels[np.abs(levels - a[p, g]) >= 10]
            a[p, g + 8] = far[np.random.randint(len(far))]
    return np.exp2(a.ravel()).repeat(32)


def f64(x):
    return np.asarray(x).astype(np.float64)


def striped(idx):
    return np.tile(idx.reshape(-1, 16).T, (8, 1)).astype(np.uint16)


def unstriped(offs):
    return offs[:16].T.reshape(-1).astype(np.int64)


E2M1 = np.array([0.0, 0.5, 1.0, 1.5, 2.0, 3.0, 4.0, 6.0, -0.0, -0.5, -1.0, -1.5, -2.0, -3.0, -4.0, -6.0])


def pack_weight(w, fmt):
    k, n = w.shape
    w = f64(np.asarray(w, np.float32).astype(ml_dtypes.bfloat16)).reshape(k // 32, 32, n)
    amax = np.abs(w).max(1)
    if fmt == "e4m3":
        byte = np.frexp(amax)[1] - 1 + 127 - 7
    else:
        mant, ex = np.frexp(amax / 6.0)
        byte = np.where(mant > 0.5, ex, ex - 1) + 127
    byte = np.clip(np.where(amax > 0, byte, 1), 1, 254)
    scaled = (w * np.exp2(127.0 - byte)[:, None, :]).reshape(k, n).astype(np.float32)
    by_word = np.ascontiguousarray(scaled.reshape(k // 512, 128, 4, n).transpose(0, 1, 3, 2))
    if fmt == "e4m3":
        words = by_word.astype(ml_dtypes.float8_e4m3fn).view(np.uint8)
    else:
        c = by_word.astype(ml_dtypes.float4_e2m1fn).view(np.uint8) & 0xF
        words = (c[..., 0::2] | (c[..., 1::2] << 4)).reshape(k // 512, 128, 2 * n)
    return np.ascontiguousarray(words), np.ascontiguousarray(byte.astype(np.uint8).reshape(k // 512, 16, n))


def unpack_weight(words, scales, fmt):
    g, _, n = scales.shape
    words = np.ascontiguousarray(words).reshape(g, 128, n, -1)
    if fmt == "e4m3":
        vals = words.view(ml_dtypes.float8_e4m3fn).astype(np.float64)
    else:
        nib = np.empty((g, 128, n, 4), np.uint8)
        nib[..., 0::2] = words & 0xF
        nib[..., 1::2] = words >> 4
        vals = E2M1[nib]
    vals = vals * np.repeat(np.exp2(scales.astype(np.float64) - 127.0), 8, axis=1)[..., None]
    return vals.transpose(0, 1, 3, 2).reshape(g * 512, n)


def gelu(v):
    return 0.5 * v * (1.0 + np.tanh(np.sqrt(2.0 / np.pi) * (v + 0.044715 * v**3)))


K, K1, T, S, H, T2, T3, S2, P = 1024, 512, 2048, 512, 1024, 1024, 2048, 512, 512

def setup_inputs():
    n = np.random.standard_normal
    s = mx_kscale(K)[:, None]
    u = mx_kscale(H)[:, None]
    tab_words, tab_scales = pack_weight(n((K, T)) * s, "e4m3")
    tab2_words, tab2_scales = pack_weight(n((H, T3)) / np.sqrt(H) / u, "e4m3")
    w4_words, w4_scales = pack_weight(1.5 * n((K - K1, H)) / np.sqrt(K) / s[K1:], "e2m1")
    return {
        "tab_words": tab_words, "tab_scales": tab_scales,
        "tab2_words": tab2_words, "tab2_scales": tab2_scales,
        "w1": (1.5 * n((K1, H)) / np.sqrt(K) / s[:K1]).astype(np.float32),
        "w4_words": w4_words, "w4_scales": w4_scales,
        "gain": (np.exp(0.3 * n(H)) * u[:, 0]).astype(np.float32),
        "wgs": np.exp(0.3 * n((128, S))).astype(np.float32),
        "page0": (0.8 * n((H, T2)) * u).astype(np.float32),
        "pipe": (0.8 * np.exp(0.4 * n(S2))).astype(np.float32),
        "offs": striped(np.random.permutation(T)[:S]),
        "offs2": striped(np.random.permutation(T3)[:S2]),
        "offs3": striped(np.random.permutation(T2)[:S]),
        "pos1": striped(np.random.permutation(T2)[:P]),
        "pos2": striped(np.random.permutation(T2)[:P]),
    }

def reference(tab_words, tab_scales, tab2_words, tab2_scales, w1, w4_words, w4_scales,
              gain, wgs, page0, pipe, offs, offs2, offs3, pos1, pos2):
    v = unpack_weight(tab_words, tab_scales, "e4m3")[:, unstriped(offs)]
    v2 = unpack_weight(tab2_words, tab2_scales, "e4m3")[:, unstriped(offs2)]
    w4 = unpack_weight(w4_words, w4_scales, "e2m1")
    w1q = mxq(f64(w1), 0, "e4m3")
    grain = w1q.T @ v[:K1] + w4.T @ v[K1:]
    h = f64(gain)[:, None] * np.tanh(grain)
    page = f64(page0).copy()
    page[:, unstriped(offs3)] = np.tile(f64(wgs), (H // 128, 1)) * h
    pageq = mxq(page, 0, "e4m3")
    e = v2.T @ pageq
    return e[:, unstriped(pos1)] - f64(pipe)[:, None] * e[:, unstriped(pos2)]

@@ -1,0 +1,239 @@
+from contextlib import ExitStack
+
+import concourse.mybir as mybir
+from concourse.masks import make_identity
+
+F32 = mybir.dt.float32
+BF16 = mybir.dt.bfloat16
+I32 = mybir.dt.int32
+U32 = mybir.dt.uint32
+U16 = mybir.dt.uint16
+U8 = mybir.dt.uint8
+FP8X4 = mybir.dt.float8_e4m3fn_x4
+FP4X4 = mybir.dt.float4_e2m1fn_x4
+ACT = mybir.ActivationFunctionType
+ALU = mybir.AluOpType
+
+P = 128
+T = 2048
+S = 512
+H = 1024
+T2 = 1024
+ROW_TILES = H // P
+PASSES = 2
+HALF = 512
+M_TILES = S // P
+W1_CHUNKS = ((0, 256), (256, 256), (512, 256), (768, 256))
+
+FLOPS = 2 * 1024 * H * S + 2 * H * S * T2
+
+
+def tile_list_grain_pipe_contrast_kernel(
+    tc, tab_words, tab_scales, tab2_words, tab2_scales, w1, w4_words, w4_scales,
+    gain, wgs, page0, pipe, offs, offs2, offs3, pos1, pos2, out,
+):
+    nc = tc.nc
+    with ExitStack() as ctx:
+        keep = ctx.enter_context(tc.tile_pool(name="keep", bufs=1))
+        psum = ctx.enter_context(tc.psum_pool(name="psum", bufs=1))
+
+        def sb(shape, dtype, name, tag=None):
+            return keep.tile(shape, dtype, name=name, tag=tag or name, align_bytes=64)
+
+        def load_list(src, name):
+            tile = keep.tile([P, S // 16], U16, name=name)
+            nc.sync.dma_start(tile[:], src)
+            return tile
+
+        def load_words(src, name):
+            tile = sb([P, T], U32, name)
+            nc.sync.dma_start(tile[:].bitcast(I32), src.rearrange("p t i -> p (t i)").bitcast(I32))
+            return tile
+
+        def gather(window, offsets, dtype, name, tag=None):
+            tile = sb([P, S], dtype, name, tag)
+            nc.vector.tensor_copy(tile[:], window.indirect(offsets[:]))
+            return tile
+
+        def load_w1(chunk):
+            first, width = W1_CHUNKS[chunk]
+            raw = sb([P, 4, width], F32, "w1_raw%d" % chunk)
+            nc.sync.dma_start(raw[:], w1[:, first:first + width].rearrange("(p j) w -> p j w", j=4))
+            return raw
+
+        def quantise_w1(chunk, raw):
+            width = W1_CHUNKS[chunk][1]
+            grouped = sb([P, 4 * width], BF16, "w1_grouped%d" % chunk, "w1_codes0" if chunk == 1 else None)
+            nc.scalar.activation(
+                grouped[:].rearrange("p (c i j) -> p c j i", i=4, j=4),
+                raw[:].rearrange("p j (c i) -> p c j i", i=4),
+                ACT.Copy,
+            )
+            codes = sb([P, width], U32, "w1_codes%d" % chunk, "h0" if chunk == 1 else None)
+            scales = sb([P, width], U8, "w1_scales%d" % chunk)
+            nc.vector.quantize_mx(codes[:].bitcast(FP8X4), scales[:], grouped[:])
+            return codes, scales
+
+        def load_page(c):
+            tile = sb([P, T2], F32, "page%d" % c)
+            nc.sync.dma_start(tile[:], page0[c * P:(c + 1) * P, :])
+            return tile
+
+        tab_sc = sb([P, PASSES * T], U8, "tab_sc")
+        nc.vector.memset(tab_sc[:].bitcast(I32), 0)
+        w4_sc = sb([P, H], U8, "w4_sc")
+        nc.vector.memset(w4_sc[:].bitcast(I32), 0)
+        tab2_sc = sb([P, T], U8, "tab2_sc")
+        nc.vector.memset(tab2_sc[:].bitcast(I32), 0)
+        rows = sb([P, P], F32, "rows")
+        nc.gpsimd.memset(rows[:], 0.0)
+        nc.gpsimd.dma_start(rows[0:ROW_TILES, :], gain.rearrange("(c p) -> c p", p=P))
+        ident = sb([P, P], F32, "ident")
+        make_identity(nc, ident[:])
+        for q in range(4):
+            nc.gpsimd.dma_start(
+                w4_sc[32 * q:32 * q + 4, :].bitcast(I32), w4_scales[0, 4 * q:4 * q + 4, :].bitcast(I32)
+            )
+
+        offs_t = load_list(offs, "offs_t")
+        offs3_t = load_list(offs3, "offs3_t")
+        offs2_t = load_list(offs2, "offs2_t")
+        pos1_t = load_list(pos1, "pos1_t")
+        pos2_t = load_list(pos2, "pos2_t")
+        for q in range(4):
+            nc.scalar.dma_start(
+                tab_sc[32 * q:32 * q + 4, :].bitcast(I32).rearrange("q (a w) -> q a w", a=PASSES),
+                tab_scales[:, 4 * q:4 * q + 4, :].bitcast(I32).rearrange("a q w -> q a w"),
+            )
+        tab_w = [load_words(tab_words[0], "tab_w0")]
+        w1_raw = [load_w1(0)]
+        tab_w.append(load_words(tab_words[1], "tab_w1"))
+        w4_w = sb([P, 2 * H], U8, "w4_w")
+        nc.sync.dma_start(w4_w[:].bitcast(I32), w4_words[0].bitcast(I32))
+        wgs_t = sb([P, S], F32, "wgs_t")
+        nc.sync.dma_start(wgs_t[:], wgs)
+        page = [load_page(0)]
+        w1_raw.append(load_w1(1))
+        w1_raw.append(load_w1(2))
+        page.append(load_page(1))
+        w1_raw.append(load_w1(3))
+        for c in range(2, 6):
+            page.append(load_page(c))
+        pipe_t = sb([P, M_TILES], F32, "pipe_t")
+        with nc.allow_non_contiguous_dma(reason="one factor a candidate, candidates on the partitions"):
+            nc.sync.dma_start(pipe_t[:], pipe.rearrange("(c p) -> p c", p=P))
+        for q in range(4):
+            nc.sync.dma_start(
+                tab2_sc[32 * q:32 * q + 4 * PASSES, :].bitcast(I32),
+                tab2_scales[:, 4 * q:4 * q + 4, :].bitcast(I32),
+            )
+        tab2_w = [load_words(tab2_words[a], "tab2_w%d" % a) for a in range(PASSES)]
+        for c in range(6, ROW_TILES):
+            page.append(load_page(c))
+
+        turned = psum.tile([P, HALF], F32, name="turned", tag="acc", bufs=4)
+        nc.tensor.transpose(turned[:, 0:P], rows[:], ident[:])
+        factors = sb([P, ROW_TILES], F32, "factors")
+        nc.scalar.copy(factors[:], turned[:, 0:ROW_TILES])
+
+        v_w = [gather(tab_w[0][:], offs_t, U32, "v_w0")]
+        v_sc = [gather(tab_sc[:, a * T:(a + 1) * T], offs_t, U8, "v_sc%d" % a) for a in range(PASSES)]
+        w1_q = [quantise_w1(0, w1_raw[0])]
+        v_w.append(gather(tab_w[1][:], offs_t, U32, "v_w1", "tab_sc"))
+
+        h = []
+        wg = []
+        for c in range(ROW_TILES):
+            chunk = max(i for i in range(len(W1_CHUNKS)) if W1_CHUNKS[i][0] <= c * P)
+            if chunk == len(w1_q):
+                w1_q.append(quantise_w1(chunk, w1_raw[chunk]))
+            codes, scales = w1_q[chunk]
+            lo = c * P - W1_CHUNKS[chunk][0]
+            wg_c = sb([P, S], F32, "wg%d" % c)
+            nc.scalar.activation(wg_c[:], wgs_t[:], ACT.Copy, scale=factors[:, c:c + 1])
+            wg.append(wg_c)
+            grain = psum.tile([P, HALF], F32, name="grain", tag="acc", bufs=4)
+            nc.tensor.matmul_mx(
+                grain[:], lhsT=codes[:, lo:lo + P].bitcast(FP8X4), lhsT_scale=scales[:, lo:lo + P],
+                rhs=v_w[0][:].bitcast(FP8X4), rhs_scale=v_sc[0][:], start=True, stop=False,
+            )
+            nc.tensor.matmul_mx(
+                grain[:], lhsT=w4_w[:, 2 * c * P:2 * (c + 1) * P].bitcast(FP4X4),
+                lhsT_scale=w4_sc[:, c * P:(c + 1) * P],
+                rhs=v_w[1][:].bitcast(FP8X4), rhs_scale=v_sc[1][:], start=False, stop=True,
+            )
+            h_c = sb([P, S], F32, "h%d" % c)
+            nc.scalar.activation(h_c[:], grain[:], ACT.Tanh)
+            h.append(h_c)
+
+        page_grouped = {}
+        for a in range(PASSES):
+            by_col = [sb([P, 4, 2, 2 * P], BF16, "by_col%d_%d" % (a, half)) for half in range(2)]
+            for cl in range(4):
+                c = 4 * a + cl
+                nc.vector.tensor_tensor(page[c][:].indirect(offs3_t[:]), h[c][:], wg[c][:], ALU.mult)
+                for half in range(2):
+                    t1 = psum.tile([P, 4, P], F32, name="t1", tag="t1", bufs=2)
+                    for nb in range(4):
+                        n0 = half * HALF + nb * P
+                        nc.tensor.transpose(t1[:, nb, :], page[c][:, n0:n0 + P], ident[:])
+                    nc.scalar.copy(
+                        by_col[half][:, :, :, 64 * cl:64 * (cl + 1)].rearrange("n b u (q e) -> n b u q e", e=2),
+                        t1[:].rearrange("n b (q u e) -> n b u q e", u=2, e=2),
+                    )
+            for half in range(2):
+                words = by_col[half][:].bitcast(F32)
+                grouped = sb([P, 2 * HALF], F32, "page_grouped%d_%d" % (a, half))
+                for pair in range(2):
+                    t2 = psum.tile([P, 2, 2, P], F32, name="t2", tag="t2", bufs=2)
+                    for nb in range(2):
+                        for u in range(2):
+                            nc.tensor.transpose(t2[:, nb, u, :], words[:, 2 * pair + nb, u, :], ident[:])
+                    nc.scalar.copy(
+                        grouped[:, pair * HALF:(pair + 1) * HALF].rearrange("p (b n u) -> p b n u", b=2, u=2),
+                        t2[:].rearrange("p b u n -> p b n u"),
+                    )
+                page_grouped[(a, half)] = grouped
+
+        v2_w = [gather(tab2_w[a][:], offs2_t, U32, "v2_w%d" % a, ("h7", "wg7")[a]) for a in range(PASSES)]
+        v2_sc = gather(tab2_sc[:], offs2_t, U8, "v2_sc", "tab2_w1")
+        page_q = {}
+        for a in range(PASSES):
+            codes = sb([P, T2], U32, "page_codes%d" % a, ("tab2_w0", "page_codes1")[a])
+            scales = sb([P, T2], U8, "page_scales%d" % a)
+            for half in range(2):
+                cols = slice(half * HALF, (half + 1) * HALF)
+                nc.vector.quantize_mx(
+                    codes[:, cols].bitcast(FP8X4), scales[:, cols], page_grouped[(a, half)][:].bitcast(BF16)
+                )
+                page_q[(a, half)] = (codes[:, cols], scales[:, cols])
+        scores = []
+        for m in range(M_TILES):
+            e = sb([P, T2], F32, "scores%d" % m)
+            for half in range(2):
+                acc = psum.tile([P, HALF], F32, name="score_acc", tag="acc", bufs=4)
+                for a in range(PASSES):
+                    codes, scales = page_q[(a, half)]
+                    nc.tensor.matmul_mx(
+                        acc[:], lhsT=v2_w[a][:, m * P:(m + 1) * P].bitcast(FP8X4),
+                        lhsT_scale=v2_sc[4 * a:P, m * P:(m + 1) * P],
+                        rhs=codes.bitcast(FP8X4), rhs_scale=scales,
+                        start=(a == 0), stop=(a == PASSES - 1),
+                    )
+                nc.scalar.copy(e[:, half * HALF:(half + 1) * HALF], acc[:])
+            scores.append(e)
+
+        down = []
+
+        def downstream(m):
+            g = gather(scores[m][:], pos2_t, F32, "down%d" % m)
+            nc.scalar.activation(g[:], g[:], ACT.Copy, scale=pipe_t[:, m:m + 1])
+            down.append(g)
+
+        downstream(0)
+        for m in range(M_TILES):
+            if m + 1 < M_TILES:
+                downstream(m + 1)
+            result = sb([P, S], F32, "result%d" % m)
+            nc.vector.tensor_tensor(result[:], scores[m][:].indirect(pos1_t[:]), down[m][:], ALU.subtract)
+            nc.sync.dma_start(out[m * P:(m + 1) * P, :], result[:])

@@ -79,8 +79,6 @@ def tile_list_grain_pipe_contrast_kernel(
             nc.sync.dma_start(tile[:], page0[c * P:(c + 1) * P, :])
             return tile
 
-        tab_sc = sb([P, PASSES * T], U8, "tab_sc")
-        nc.vector.memset(tab_sc[:].bitcast(I32), 0)
         w4_sc = sb([P, H], U8, "w4_sc")
         nc.vector.memset(w4_sc[:].bitcast(I32), 0)
         tab2_sc = sb([P, T], U8, "tab2_sc")
@@ -90,26 +88,22 @@ def tile_list_grain_pipe_contrast_kernel(
         nc.gpsimd.dma_start(rows[0:ROW_TILES, :], gain.rearrange("(c p) -> c p", p=P))
         ident = sb([P, P], F32, "ident")
         make_identity(nc, ident[:])
-        for q in range(4):
-            nc.gpsimd.dma_start(
-                w4_sc[32 * q:32 * q + 4, :].bitcast(I32), w4_scales[0, 4 * q:4 * q + 4, :].bitcast(I32)
-            )
 
         offs_t = load_list(offs, "offs_t")
         offs3_t = load_list(offs3, "offs3_t")
-        offs2_t = load_list(offs2, "offs2_t")
-        pos1_t = load_list(pos1, "pos1_t")
-        pos2_t = load_list(pos2, "pos2_t")
-        for q in range(4):
-            nc.scalar.dma_start(
-                tab_sc[32 * q:32 * q + 4, :].bitcast(I32).rearrange("q (a w) -> q a w", a=PASSES),
-                tab_scales[:, 4 * q:4 * q + 4, :].bitcast(I32).rearrange("a q w -> q a w"),
-            )
         tab_w = [load_words(tab_words[0], "tab_w0")]
         w1_raw = [load_w1(0)]
+        tab_sc = sb([P, T], U8, "tab_sc")
+        scale_rows = tab_scales.rearrange("a q t -> (a q) t").bitcast(I32)
+        for first, last, row in ((0, 12, 16), (12, 44, 0), (44, 72, 4), (72, 100, 4), (100, 128, 4)):
+            nc.sync.dma_start(tab_sc[first:last, :].bitcast(I32), scale_rows[row:row + last - first, :])
         tab_w.append(load_words(tab_words[1], "tab_w1"))
         w4_w = sb([P, 2 * H], U8, "w4_w")
         nc.sync.dma_start(w4_w[:].bitcast(I32), w4_words[0].bitcast(I32))
+        for q in range(4):
+            nc.sync.dma_start(
+                w4_sc[32 * q:32 * q + 4, :].bitcast(I32), w4_scales[0, 4 * q:4 * q + 4, :].bitcast(I32)
+            )
         wgs_t = sb([P, S], F32, "wgs_t")
         nc.sync.dma_start(wgs_t[:], wgs)
         page = [load_page(0)]
@@ -119,6 +113,9 @@ def tile_list_grain_pipe_contrast_kernel(
         w1_raw.append(load_w1(3))
         for c in range(2, 6):
             page.append(load_page(c))
+        offs2_t = load_list(offs2, "offs2_t")
+        pos1_t = load_list(pos1, "pos1_t")
+        pos2_t = load_list(pos2, "pos2_t")
         pipe_t = sb([P, M_TILES], F32, "pipe_t")
         with nc.allow_non_contiguous_dma(reason="one factor a candidate, candidates on the partitions"):
             nc.sync.dma_start(pipe_t[:], pipe.rearrange("(c p) -> p c", p=P))
@@ -137,7 +134,7 @@ def tile_list_grain_pipe_contrast_kernel(
         nc.scalar.copy(factors[:], turned[:, 0:ROW_TILES])
 
         v_w = [gather(tab_w[0][:], offs_t, U32, "v_w0")]
-        v_sc = [gather(tab_sc[:, a * T:(a + 1) * T], offs_t, U8, "v_sc%d" % a) for a in range(PASSES)]
+        v_sc = gather(tab_sc[:], offs_t, U8, "v_sc")
         w1_q = [quantise_w1(0, w1_raw[0])]
         v_w.append(gather(tab_w[1][:], offs_t, U32, "v_w1", "tab_sc"))
 
@@ -155,12 +152,12 @@ def tile_list_grain_pipe_contrast_kernel(
             grain = psum.tile([P, HALF], F32, name="grain", tag="acc", bufs=4)
             nc.tensor.matmul_mx(
                 grain[:], lhsT=codes[:, lo:lo + P].bitcast(FP8X4), lhsT_scale=scales[:, lo:lo + P],
-                rhs=v_w[0][:].bitcast(FP8X4), rhs_scale=v_sc[0][:], start=True, stop=False,
+                rhs=v_w[0][:].bitcast(FP8X4), rhs_scale=v_sc[12:P, :], start=True, stop=False,
             )
             nc.tensor.matmul_mx(
                 grain[:], lhsT=w4_w[:, 2 * c * P:2 * (c + 1) * P].bitcast(FP4X4),
                 lhsT_scale=w4_sc[:, c * P:(c + 1) * P],
-                rhs=v_w[1][:].bitcast(FP8X4), rhs_scale=v_sc[1][:], start=False, stop=True,
+                rhs=v_w[1][:].bitcast(FP8X4), rhs_scale=v_sc[:], start=False, stop=True,
             )
             h_c = sb([P, S], F32, "h%d" % c)
             nc.scalar.activation(h_c[:], grain[:], ACT.Tanh)
@@ -195,30 +192,37 @@ def tile_list_grain_pipe_contrast_kernel(
                     )
                 page_grouped[(a, half)] = grouped
 
-        v2_w = [gather(tab2_w[a][:], offs2_t, U32, "v2_w%d" % a, ("h7", "wg7")[a]) for a in range(PASSES)]
-        v2_sc = gather(tab2_sc[:], offs2_t, U8, "v2_sc", "tab2_w1")
+        def gather_candidates(part, word_tag, scale_tag):
+            entries = offs2_t[:, part * 16:(part + 1) * 16]
+            words = sb([P, PASSES, S // 2], U32, "v2_w%d" % part, word_tag)
+            for a in range(PASSES):
+                nc.vector.tensor_copy(words[:, a, :], tab2_w[a][:].indirect(entries))
+            scales = sb([P, S // 2], U8, "v2_sc%d" % part, scale_tag)
+            nc.vector.tensor_copy(scales[:], tab2_sc[:].indirect(entries))
+            return words, scales
+
+        v2 = [gather_candidates(0, "h7", "h6")]
         page_q = {}
         for a in range(PASSES):
-            codes = sb([P, T2], U32, "page_codes%d" % a, ("tab2_w0", "page_codes1")[a])
-            scales = sb([P, T2], U8, "page_scales%d" % a)
             for half in range(2):
-                cols = slice(half * HALF, (half + 1) * HALF)
-                nc.vector.quantize_mx(
-                    codes[:, cols].bitcast(FP8X4), scales[:, cols], page_grouped[(a, half)][:].bitcast(BF16)
-                )
-                page_q[(a, half)] = (codes[:, cols], scales[:, cols])
+                codes = sb([P, HALF], U32, "page_codes%d_%d" % (a, half), ("wg7", "page7")[half] if a == 0 else None)
+                scales = sb([P, HALF], U8, "page_scales%d_%d" % (a, half))
+                nc.vector.quantize_mx(codes[:].bitcast(FP8X4), scales[:], page_grouped[(a, half)][:].bitcast(BF16))
+                page_q[(a, half)] = (codes, scales)
+        v2.append(gather_candidates(1, "page_grouped1_1", "page_grouped1_0"))
         scores = []
         for m in range(M_TILES):
             e = sb([P, T2], F32, "scores%d" % m)
+            v2_w, v2_sc = v2[m // 2]
+            cols = slice(m % 2 * P, (m % 2 + 1) * P)
             for half in range(2):
                 acc = psum.tile([P, HALF], F32, name="score_acc", tag="acc", bufs=4)
-                for a in range(PASSES):
+                for a in (1, 0):
                     codes, scales = page_q[(a, half)]
                     nc.tensor.matmul_mx(
-                        acc[:], lhsT=v2_w[a][:, m * P:(m + 1) * P].bitcast(FP8X4),
-                        lhsT_scale=v2_sc[4 * a:P, m * P:(m + 1) * P],
-                        rhs=codes.bitcast(FP8X4), rhs_scale=scales,
-                        start=(a == 0), stop=(a == PASSES - 1),
+                        acc[:], lhsT=v2_w[:, a, cols].bitcast(FP8X4), lhsT_scale=v2_sc[4 * a:P, cols],
+                        rhs=codes[:].bitcast(FP8X4), rhs_scale=scales[:],
+                        start=(a == 1), stop=(a == 0),
                     )
                 nc.scalar.copy(e[:, half * HALF:(half + 1) * HALF], acc[:])
             scores.append(e)

@@ -25,6 +25,8 @@ HALF = 512
 M_TILES = S // P
 W1_CHUNKS = ((0, 256), (256, 256), (512, 256), (768, 256))
 
+W4_FIRST = 512
+
 FLOPS = 2 * 1024 * H * S + 2 * H * S * T2
 
 
@@ -63,13 +65,13 @@ def tile_list_grain_pipe_contrast_kernel(
 
         def quantise_w1(chunk, raw):
             width = W1_CHUNKS[chunk][1]
-            grouped = sb([P, 4 * width], BF16, "w1_grouped%d" % chunk, "w1_codes0" if chunk == 1 else None)
+            grouped = sb([P, 4 * width], BF16, "w1_grouped%d" % chunk, (None, "w1_codes0", "w1_scales0", "w1_codes0")[chunk])
             nc.scalar.activation(
                 grouped[:].rearrange("p (c i j) -> p c j i", i=4, j=4),
                 raw[:].rearrange("p j (c i) -> p c j i", i=4),
                 ACT.Copy,
             )
-            codes = sb([P, width], U32, "w1_codes%d" % chunk, "h0" if chunk == 1 else None)
+            codes = sb([P, width], U32, "w1_codes%d" % chunk, "h%d" % (chunk - 1) if chunk > 0 else None)
             scales = sb([P, width], U8, "w1_scales%d" % chunk)
             nc.vector.quantize_mx(codes[:].bitcast(FP8X4), scales[:], grouped[:])
             return codes, scales
@@ -97,17 +99,18 @@ def tile_list_grain_pipe_contrast_kernel(
         scale_rows = tab_scales.rearrange("a q t -> (a q) t").bitcast(I32)
         for first, last, row in ((0, 12, 16), (12, 44, 0), (44, 72, 4), (72, 100, 4), (100, 128, 4)):
             nc.sync.dma_start(tab_sc[first:last, :].bitcast(I32), scale_rows[row:row + last - first, :])
+        wgs_t = sb([P, S], F32, "wgs_t")
+        nc.sync.dma_start(wgs_t[:], wgs)
         tab_w.append(load_words(tab_words[1], "tab_w1"))
         w4_w = sb([P, 2 * H], U8, "w4_w")
-        nc.sync.dma_start(w4_w[:].bitcast(I32), w4_words[0].bitcast(I32))
+        nc.sync.dma_start(w4_w[:, 0:W4_FIRST].bitcast(I32), w4_words[0, :, 0:W4_FIRST].bitcast(I32))
         for q in range(4):
             nc.sync.dma_start(
                 w4_sc[32 * q:32 * q + 4, :].bitcast(I32), w4_scales[0, 4 * q:4 * q + 4, :].bitcast(I32)
             )
-        wgs_t = sb([P, S], F32, "wgs_t")
-        nc.sync.dma_start(wgs_t[:], wgs)
         page = [load_page(0)]
         w1_raw.append(load_w1(1))
+        nc.sync.dma_start(w4_w[:, W4_FIRST:].bitcast(I32), w4_words[0, :, W4_FIRST:].bitcast(I32))
         w1_raw.append(load_w1(2))
         page.append(load_page(1))
         w1_raw.append(load_w1(3))
@@ -136,7 +139,11 @@ def tile_list_grain_pipe_contrast_kernel(
         v_w = [gather(tab_w[0][:], offs_t, U32, "v_w0")]
         v_sc = gather(tab_sc[:], offs_t, U8, "v_sc")
         w1_q = [quantise_w1(0, w1_raw[0])]
-        v_w.append(gather(tab_w[1][:], offs_t, U32, "v_w1", "tab_sc"))
+        v_w.append(sb([P, S], U32, "v_w1", "tab_sc"))
+        for part in range(2):
+            nc.vector.tensor_copy(
+                v_w[1][:, part * 256:(part + 1) * 256], tab_w[1][:].indirect(offs_t[:, part * 16:(part + 1) * 16])
+            )
 
         h = []
         wg = []
@@ -149,18 +156,22 @@ def tile_list_grain_pipe_contrast_kernel(
             wg_c = sb([P, S], F32, "wg%d" % c)
             nc.scalar.activation(wg_c[:], wgs_t[:], ACT.Copy, scale=factors[:, c:c + 1])
             wg.append(wg_c)
-            grain = psum.tile([P, HALF], F32, name="grain", tag="acc", bufs=4)
-            nc.tensor.matmul_mx(
-                grain[:], lhsT=codes[:, lo:lo + P].bitcast(FP8X4), lhsT_scale=scales[:, lo:lo + P],
-                rhs=v_w[0][:].bitcast(FP8X4), rhs_scale=v_sc[12:P, :], start=True, stop=False,
-            )
-            nc.tensor.matmul_mx(
-                grain[:], lhsT=w4_w[:, 2 * c * P:2 * (c + 1) * P].bitcast(FP4X4),
-                lhsT_scale=w4_sc[:, c * P:(c + 1) * P],
-                rhs=v_w[1][:].bitcast(FP8X4), rhs_scale=v_sc[:], start=False, stop=True,
-            )
             h_c = sb([P, S], F32, "h%d" % c)
-            nc.scalar.activation(h_c[:], grain[:], ACT.Tanh)
+            for j in ((slice(0, 256), slice(256, S)) if c == 0 else (slice(0, S),)):
+                if c in (2, 3):
+                    grain = psum.tile([P, HALF], F32, name="grain", tag="t1", bufs=2)
+                else:
+                    grain = psum.tile([P, HALF], F32, name="grain", tag="acc", bufs=4)
+                nc.tensor.matmul_mx(
+                    grain[:, j], lhsT=codes[:, lo:lo + P].bitcast(FP8X4), lhsT_scale=scales[:, lo:lo + P],
+                    rhs=v_w[0][:, j].bitcast(FP8X4), rhs_scale=v_sc[12:P, j], start=True, stop=False,
+                )
+                nc.tensor.matmul_mx(
+                    grain[:, j], lhsT=w4_w[:, 2 * c * P:2 * (c + 1) * P].bitcast(FP4X4),
+                    lhsT_scale=w4_sc[:, c * P:(c + 1) * P],
+                    rhs=v_w[1][:, j].bitcast(FP8X4), rhs_scale=v_sc[:, j], start=False, stop=True,
+                )
+                nc.scalar.activation(h_c[:, j], grain[:, j], ACT.Tanh)
             h.append(h_c)
 
         page_grouped = {}
@@ -168,7 +179,9 @@ def tile_list_grain_pipe_contrast_kernel(
             by_col = [sb([P, 4, 2, 2 * P], BF16, "by_col%d_%d" % (a, half)) for half in range(2)]
             for cl in range(4):
                 c = 4 * a + cl
-                nc.vector.tensor_tensor(page[c][:].indirect(offs3_t[:]), h[c][:], wg[c][:], ALU.mult)
+                for j in ((slice(0, 256), slice(256, S)) if c == 0 else (slice(0, S),)):
+                    entries = offs3_t[:, j.start // 16:j.stop // 16]
+                    nc.vector.tensor_tensor(page[c][:].indirect(entries), h[c][:, j], wg[c][:, j], ALU.mult)
                 for half in range(2):
                     t1 = psum.tile([P, 4, P], F32, name="t1", tag="t1", bufs=2)
                     for nb in range(4):
@@ -216,13 +229,17 @@ def tile_list_grain_pipe_contrast_kernel(
             v2_w, v2_sc = v2[m // 2]
             cols = slice(m % 2 * P, (m % 2 + 1) * P)
             for half in range(2):
-                acc = psum.tile([P, HALF], F32, name="score_acc", tag="acc", bufs=4)
-                for a in (1, 0):
+                if m == 0:
+                    acc = psum.tile([P, HALF], F32, name="score_acc", tag="t2", bufs=2)
+                else:
+                    acc = psum.tile([P, HALF], F32, name="score_acc", tag="acc", bufs=4)
+                order = (0, 1) if m == 0 else (1, 0)
+                for a in order:
                     codes, scales = page_q[(a, half)]
                     nc.tensor.matmul_mx(
                         acc[:], lhsT=v2_w[:, a, cols].bitcast(FP8X4), lhsT_scale=v2_sc[4 * a:P, cols],
                         rhs=codes[:].bitcast(FP8X4), rhs_scale=scales[:],
-                        start=(a == 1), stop=(a == 0),
+                        start=(a == order[0]), stop=(a == order[1]),
                     )
                 nc.scalar.copy(e[:, half * HALF:(half + 1) * HALF], acc[:])
             scores.append(e)
@@ -239,5 +256,7 @@ def tile_list_grain_pipe_contrast_kernel(
             if m + 1 < M_TILES:
                 downstream(m + 1)
             result = sb([P, S], F32, "result%d" % m)
-            nc.vector.tensor_tensor(result[:], scores[m][:].indirect(pos1_t[:]), down[m][:], ALU.subtract)
-            nc.sync.dma_start(out[m * P:(m + 1) * P, :], result[:])
+            for j in ((slice(0, 256), slice(256, S)) if m == M_TILES - 1 else (slice(0, S),)):
+                entries = pos1_t[:, j.start // 16:j.stop // 16]
+                nc.vector.tensor_tensor(result[:, j], scores[m][:].indirect(entries), down[m][:, j], ALU.subtract)
+                nc.sync.dma_start(out[m * P:(m + 1) * P, j], result[:, j])

from contextlib import ExitStack

import concourse.mybir as mybir
from concourse.masks import make_identity

F32 = mybir.dt.float32
BF16 = mybir.dt.bfloat16
I32 = mybir.dt.int32
U32 = mybir.dt.uint32
U16 = mybir.dt.uint16
U8 = mybir.dt.uint8
FP8X4 = mybir.dt.float8_e4m3fn_x4
FP4X4 = mybir.dt.float4_e2m1fn_x4
ACT = mybir.ActivationFunctionType
ALU = mybir.AluOpType

P = 128
T = 2048
S = 512
H = 1024
T2 = 1024
ROW_TILES = H // P
PASSES = 2
HALF = 512
M_TILES = S // P
W1_CHUNKS = ((0, 256), (256, 256), (512, 256), (768, 256))

W4_FIRST = 512

FLOPS = 2 * 1024 * H * S + 2 * H * S * T2


def tile_list_grain_pipe_contrast_kernel(
    tc, tab_words, tab_scales, tab2_words, tab2_scales, w1, w4_words, w4_scales,
    gain, wgs, page0, pipe, offs, offs2, offs3, pos1, pos2, out,
):
    nc = tc.nc
    with ExitStack() as ctx:
        keep = ctx.enter_context(tc.tile_pool(name="keep", bufs=1))
        psum = ctx.enter_context(tc.psum_pool(name="psum", bufs=1))

        def sb(shape, dtype, name, tag=None):
            return keep.tile(shape, dtype, name=name, tag=tag or name, align_bytes=64)

        def load_list(src, name):
            tile = keep.tile([P, S // 16], U16, name=name)
            nc.sync.dma_start(tile[:], src)
            return tile

        def load_words(src, name):
            tile = sb([P, T], U32, name)
            nc.sync.dma_start(tile[:].bitcast(I32), src.rearrange("p t i -> p (t i)").bitcast(I32))
            return tile

        def gather(window, offsets, dtype, name, tag=None):
            tile = sb([P, S], dtype, name, tag)
            nc.vector.tensor_copy(tile[:], window.indirect(offsets[:]))
            return tile

        def load_w1(chunk):
            first, width = W1_CHUNKS[chunk]
            raw = sb([P, 4, width], F32, "w1_raw%d" % chunk)
            nc.sync.dma_start(raw[:], w1[:, first:first + width].rearrange("(p j) w -> p j w", j=4))
            return raw

        def quantise_w1(chunk, raw):
            width = W1_CHUNKS[chunk][1]
            grouped = sb([P, 4 * width], BF16, "w1_grouped%d" % chunk, (None, "w1_codes0", "w1_scales0", "w1_codes0")[chunk])
            nc.scalar.activation(
                grouped[:].rearrange("p (c i j) -> p c j i", i=4, j=4),
                raw[:].rearrange("p j (c i) -> p c j i", i=4),
                ACT.Copy,
            )
            codes = sb([P, width], U32, "w1_codes%d" % chunk, "h%d" % (chunk - 1) if chunk > 0 else None)
            scales = sb([P, width], U8, "w1_scales%d" % chunk)
            nc.vector.quantize_mx(codes[:].bitcast(FP8X4), scales[:], grouped[:])
            return codes, scales

        def load_page(c):
            tile = sb([P, T2], F32, "page%d" % c)
            nc.sync.dma_start(tile[:], page0[c * P:(c + 1) * P, :])
            return tile

        w4_sc = sb([P, H], U8, "w4_sc")
        nc.vector.memset(w4_sc[:].bitcast(I32), 0)
        tab2_sc = sb([P, T], U8, "tab2_sc")
        nc.vector.memset(tab2_sc[:].bitcast(I32), 0)
        rows = sb([P, P], F32, "rows")
        nc.gpsimd.memset(rows[:], 0.0)
        nc.gpsimd.dma_start(rows[0:ROW_TILES, :], gain.rearrange("(c p) -> c p", p=P))
        ident = sb([P, P], F32, "ident")
        make_identity(nc, ident[:])

        offs_t = load_list(offs, "offs_t")
        offs3_t = load_list(offs3, "offs3_t")
        tab_w = [load_words(tab_words[0], "tab_w0")]
        w1_raw = [load_w1(0)]
        tab_sc = sb([P, T], U8, "tab_sc")
        scale_rows = tab_scales.rearrange("a q t -> (a q) t").bitcast(I32)
        for first, last, row in ((0, 12, 16), (12, 44, 0), (44, 72, 4), (72, 100, 4), (100, 128, 4)):
            nc.sync.dma_start(tab_sc[first:last, :].bitcast(I32), scale_rows[row:row + last - first, :])
        wgs_t = sb([P, S], F32, "wgs_t")
        nc.sync.dma_start(wgs_t[:], wgs)
        tab_w.append(load_words(tab_words[1], "tab_w1"))
        w4_w = sb([P, 2 * H], U8, "w4_w")
        nc.sync.dma_start(w4_w[:, 0:W4_FIRST].bitcast(I32), w4_words[0, :, 0:W4_FIRST].bitcast(I32))
        for q in range(4):
            nc.sync.dma_start(
                w4_sc[32 * q:32 * q + 4, :].bitcast(I32), w4_scales[0, 4 * q:4 * q + 4, :].bitcast(I32)
            )
        page = [load_page(0)]
        w1_raw.append(load_w1(1))
        nc.sync.dma_start(w4_w[:, W4_FIRST:].bitcast(I32), w4_words[0, :, W4_FIRST:].bitcast(I32))
        w1_raw.append(load_w1(2))
        page.append(load_page(1))
        w1_raw.append(load_w1(3))
        for c in range(2, 6):
            page.append(load_page(c))
        offs2_t = load_list(offs2, "offs2_t")
        pos1_t = load_list(pos1, "pos1_t")
        pos2_t = load_list(pos2, "pos2_t")
        pipe_t = sb([P, M_TILES], F32, "pipe_t")
        with nc.allow_non_contiguous_dma(reason="one factor a candidate, candidates on the partitions"):
            nc.sync.dma_start(pipe_t[:], pipe.rearrange("(c p) -> p c", p=P))
        for q in range(4):
            nc.sync.dma_start(
                tab2_sc[32 * q:32 * q + 4 * PASSES, :].bitcast(I32),
                tab2_scales[:, 4 * q:4 * q + 4, :].bitcast(I32),
            )
        tab2_w = [load_words(tab2_words[a], "tab2_w%d" % a) for a in range(PASSES)]
        for c in range(6, ROW_TILES):
            page.append(load_page(c))

        turned = psum.tile([P, HALF], F32, name="turned", tag="acc", bufs=4)
        nc.tensor.transpose(turned[:, 0:P], rows[:], ident[:])
        factors = sb([P, ROW_TILES], F32, "factors")
        nc.scalar.copy(factors[:], turned[:, 0:ROW_TILES])

        v_w = [gather(tab_w[0][:], offs_t, U32, "v_w0")]
        v_sc = gather(tab_sc[:], offs_t, U8, "v_sc")
        w1_q = [quantise_w1(0, w1_raw[0])]
        v_w.append(sb([P, S], U32, "v_w1", "tab_sc"))
        for part in range(2):
            nc.vector.tensor_copy(
                v_w[1][:, part * 256:(part + 1) * 256], tab_w[1][:].indirect(offs_t[:, part * 16:(part + 1) * 16])
            )

        h = []
        wg = []
        for c in range(ROW_TILES):
            chunk = max(i for i in range(len(W1_CHUNKS)) if W1_CHUNKS[i][0] <= c * P)
            if chunk == len(w1_q):
                w1_q.append(quantise_w1(chunk, w1_raw[chunk]))
            codes, scales = w1_q[chunk]
            lo = c * P - W1_CHUNKS[chunk][0]
            wg_c = sb([P, S], F32, "wg%d" % c)
            nc.scalar.activation(wg_c[:], wgs_t[:], ACT.Copy, scale=factors[:, c:c + 1])
            wg.append(wg_c)
            h_c = sb([P, S], F32, "h%d" % c)
            for j in ((slice(0, 256), slice(256, S)) if c == 0 else (slice(0, S),)):
                if c in (2, 3):
                    grain = psum.tile([P, HALF], F32, name="grain", tag="t1", bufs=2)
                else:
                    grain = psum.tile([P, HALF], F32, name="grain", tag="acc", bufs=4)
                nc.tensor.matmul_mx(
                    grain[:, j], lhsT=codes[:, lo:lo + P].bitcast(FP8X4), lhsT_scale=scales[:, lo:lo + P],
                    rhs=v_w[0][:, j].bitcast(FP8X4), rhs_scale=v_sc[12:P, j], start=True, stop=False,
                )
                nc.tensor.matmul_mx(
                    grain[:, j], lhsT=w4_w[:, 2 * c * P:2 * (c + 1) * P].bitcast(FP4X4),
                    lhsT_scale=w4_sc[:, c * P:(c + 1) * P],
                    rhs=v_w[1][:, j].bitcast(FP8X4), rhs_scale=v_sc[:, j], start=False, stop=True,
                )
                nc.scalar.activation(h_c[:, j], grain[:, j], ACT.Tanh)
            h.append(h_c)

        page_grouped = {}
        for a in range(PASSES):
            by_col = [sb([P, 4, 2, 2 * P], BF16, "by_col%d_%d" % (a, half)) for half in range(2)]
            for cl in range(4):
                c = 4 * a + cl
                for j in ((slice(0, 256), slice(256, S)) if c == 0 else (slice(0, S),)):
                    entries = offs3_t[:, j.start // 16:j.stop // 16]
                    nc.vector.tensor_tensor(page[c][:].indirect(entries), h[c][:, j], wg[c][:, j], ALU.mult)
                for half in range(2):
                    t1 = psum.tile([P, 4, P], F32, name="t1", tag="t1", bufs=2)
                    for nb in range(4):
                        n0 = half * HALF + nb * P
                        nc.tensor.transpose(t1[:, nb, :], page[c][:, n0:n0 + P], ident[:])
                    nc.scalar.copy(
                        by_col[half][:, :, :, 64 * cl:64 * (cl + 1)].rearrange("n b u (q e) -> n b u q e", e=2),
                        t1[:].rearrange("n b (q u e) -> n b u q e", u=2, e=2),
                    )
            for half in range(2):
                words = by_col[half][:].bitcast(F32)
                grouped = sb([P, 2 * HALF], F32, "page_grouped%d_%d" % (a, half))
                for pair in range(2):
                    t2 = psum.tile([P, 2, 2, P], F32, name="t2", tag="t2", bufs=2)
                    for nb in range(2):
                        for u in range(2):
                            nc.tensor.transpose(t2[:, nb, u, :], words[:, 2 * pair + nb, u, :], ident[:])
                    nc.scalar.copy(
                        grouped[:, pair * HALF:(pair + 1) * HALF].rearrange("p (b n u) -> p b n u", b=2, u=2),
                        t2[:].rearrange("p b u n -> p b n u"),
                    )
                page_grouped[(a, half)] = grouped

        def gather_candidates(part, word_tag, scale_tag):
            entries = offs2_t[:, part * 16:(part + 1) * 16]
            words = sb([P, PASSES, S // 2], U32, "v2_w%d" % part, word_tag)
            for a in range(PASSES):
                nc.vector.tensor_copy(words[:, a, :], tab2_w[a][:].indirect(entries))
            scales = sb([P, S // 2], U8, "v2_sc%d" % part, scale_tag)
            nc.vector.tensor_copy(scales[:], tab2_sc[:].indirect(entries))
            return words, scales

        v2 = [gather_candidates(0, "h7", "h6")]
        page_q = {}
        for a in range(PASSES):
            for half in range(2):
                codes = sb([P, HALF], U32, "page_codes%d_%d" % (a, half), ("wg7", "page7")[half] if a == 0 else None)
                scales = sb([P, HALF], U8, "page_scales%d_%d" % (a, half))
                nc.vector.quantize_mx(codes[:].bitcast(FP8X4), scales[:], page_grouped[(a, half)][:].bitcast(BF16))
                page_q[(a, half)] = (codes, scales)
        v2.append(gather_candidates(1, "page_grouped1_1", "page_grouped1_0"))
        scores = []
        for m in range(M_TILES):
            e = sb([P, T2], F32, "scores%d" % m)
            v2_w, v2_sc = v2[m // 2]
            cols = slice(m % 2 * P, (m % 2 + 1) * P)
            for half in range(2):
                if m == 0:
                    acc = psum.tile([P, HALF], F32, name="score_acc", tag="t2", bufs=2)
                else:
                    acc = psum.tile([P, HALF], F32, name="score_acc", tag="acc", bufs=4)
                order = (0, 1) if m == 0 else (1, 0)
                for a in order:
                    codes, scales = page_q[(a, half)]
                    nc.tensor.matmul_mx(
                        acc[:], lhsT=v2_w[:, a, cols].bitcast(FP8X4), lhsT_scale=v2_sc[4 * a:P, cols],
                        rhs=codes[:].bitcast(FP8X4), rhs_scale=scales[:],
                        start=(a == order[0]), stop=(a == order[1]),
                    )
                nc.scalar.copy(e[:, half * HALF:(half + 1) * HALF], acc[:])
            scores.append(e)

        down = []

        def downstream(m):
            g = gather(scores[m][:], pos2_t, F32, "down%d" % m)
            nc.scalar.activation(g[:], g[:], ACT.Copy, scale=pipe_t[:, m:m + 1])
            down.append(g)

        downstream(0)
        for m in range(M_TILES):
            if m + 1 < M_TILES:
                downstream(m + 1)
            result = sb([P, S], F32, "result%d" % m)
            for j in ((slice(0, 256), slice(256, S)) if m == M_TILES - 1 else (slice(0, S),)):
                entries = pos1_t[:, j.start // 16:j.stop // 16]
                nc.vector.tensor_tensor(result[:, j], scores[m][:].indirect(entries), down[m][:, j], ALU.subtract)
                nc.sync.dma_start(out[m * P:(m + 1) * P, j], result[:, j])
